import numpy as np
import ml_dtypes


def mxq(x, axis, fmt="e4m3"):
    dtype, down = {"e4m3": (ml_dtypes.float8_e4m3fn, 7), "e5m2": (ml_dtypes.float8_e5m2, 14)}[fmt]
    v = np.moveaxis(np.asarray(x, np.float32).astype(ml_dtypes.bfloat16).astype(np.float64), axis, -1)
    blocks = v.reshape(v.shape[:-1] + (-1, 32))
    amax = np.abs(blocks).max(-1, keepdims=True)
    byte = np.maximum(np.where(amax > 0, np.frexp(amax)[1] - 1 + 127, 0) - down, 1)
    scale = np.exp2(byte - 127.0)
    codes = (blocks / scale).astype(np.float32).astype(dtype).astype(np.float64)
    return np.moveaxis((codes * scale).reshape(v.shape), -1, axis)


WIDE = False


def mx_kscale(k):
    if not WIDE:
        return np.ones(k)
    levels = np.array([10, -10, 5, -5, 0])
    if k % 512:
        return np.exp2(np.random.permutation(np.resize(levels, k // 32))).repeat(32)
    a = np.empty((k // 512, 16))
    for p in range(k // 512):
        a[p, :8] = np.random.permutation(np.resize(levels, 8))
        for g in range(8):
            far = levels[np.abs(levels - a[p, g]) >= 10]
            a[p, g + 8] = far[np.random.randint(len(far))]
    return np.exp2(a.ravel()).repeat(32)


BF16 = ml_dtypes.bfloat16


def bf(x):
    return np.asarray(x, np.float32).astype(BF16)


def f64(x):
    return np.asarray(x).astype(np.float64)


H, S, K, D, R = 2, 4096, 512, 512, 256


def draw0():
    s, t, r = mx_kscale(K), mx_kscale(D), mx_kscale(K)
    k = np.random.standard_normal((H, S, K)) * s
    mq = np.random.standard_normal((H, K)) * 0.6 / s
    wq = np.random.standard_normal((H, K, D)) / np.sqrt(K) / s[:, None] * t
    l = np.random.standard_normal((D, R)) * 0.6 * K**0.25 / np.sqrt(D) / t[:, None]
    v = np.random.standard_normal((H, S, K)) * r
    wo = np.random.standard_normal((H, K, D)) / np.sqrt(K) / r[:, None]
    return {"k": bf(k), "mq": bf(mq), "wq": bf(wq), "l": bf(l), "v": bf(v), "wo": bf(wo)}


def expected_logits(k, mq, z):
    key_dim = k.shape[-1]
    mean_term = np.sum(k * mq[:, None, :], axis=-1) / np.sqrt(key_dim)
    var_term = 0.5 * np.sum(np.square(z), axis=-1) / key_dim
    return mean_term + var_term


def core(k, mq, wq, l, v, wo):
    seq_len = k.shape[1]
    u = mxq(f64(k), 2, "e4m3") @ mxq(f64(wq), 1, "e4m3")
    z = mxq(u, 2, "e4m3") @ mxq(f64(l), 0, "e4m3")
    e = expected_logits(f64(k), f64(mq), z)
    p = np.exp(e - e.max(-1, keepdims=True))
    a = seq_len * (p / p.sum(-1, keepdims=True))
    y = mxq(f64(v), 2, "e4m3") @ mxq(f64(wo), 1, "e4m3")
    return a[:, :, None] * y


def e4m3fn_bytes(y):
    return np.clip(np.asarray(y, np.float64), -448.0, 448.0).astype(np.float32).astype(ml_dtypes.float8_e4m3fn).view(np.uint8)


def e4m3fn_values(b):
    return np.asarray(b, np.uint8).view(ml_dtypes.float8_e4m3fn).astype(np.float64)


def setup_inputs():
    d = draw0()
    x0 = np.asarray(d['v']).astype(np.float64)
    s = (np.max(np.abs(x0), axis=(0, 1), keepdims=True) / 448.0).astype(np.float32)
    out = {}
    for k, v in d.items():
        if k == 'v':
            out['v_bytes'] = e4m3fn_bytes(x0 / s.astype(np.float64))
            out['v_scale'] = s
        else:
            out[k] = v
    return out


def reference(k, mq, wq, l, v_bytes, v_scale, wo):
    return core(k, mq, wq, l, e4m3fn_values(v_bytes) * v_scale.astype(np.float64), wo)

from contextlib import ExitStack

import concourse.mybir as mybir
from concourse.masks import make_identity

H, S, K, D, R = 2, 4096, 512, 512, 256
FLOPS = 2 * H * S * (K * D + D * R + K * D + K)
BYTES = H * S * K * 2 + H * K * 2 + 2 * H * K * D * 2 + D * R * 2 + H * S * K + K * 4 + H * S * D * 4

F32 = mybir.dt.float32
BF16 = mybir.dt.bfloat16
U32 = mybir.dt.uint32
U8 = mybir.dt.uint8
FP8 = mybir.dt.float8_e4m3fn
FP8X4 = mybir.dt.float8_e4m3fn_x4
ACT = mybir.ActivationFunctionType
ALU = mybir.AluOpType
AX = mybir.AxisListType

P = 128
TILES = S // P
PAIRS = H * TILES // 2
HEAD_PAIRS = PAIRS // H
GROUP = 4
MEAN_N = 64
L_X = 2
L_U = 2
L_Z = 2
L_Y = 3
LIMIT = {"x": L_X, "ue": L_U, "zs": L_Z, "ye": L_Y}
G_BUFS = 5
VB_BUFS = 3
UG_BUFS = 4
O_BUFS = 5
MEAN_W = 391
HOP = 138
HOP_P = 171
ADJACENT = 253
SWITCH = 50
SWITCH_DUE = 118
SLACK = 0
V_BIAS = 447
K_STEP = 2013
V0 = 6221
V_STEP = 4874
V_BEND = 16
V_STEP2 = 1100
Y0 = 62722
Y_STEP = 1736
Y1 = 72651
Y_STEP2 = 1348


def tile_expectedattentionlatentkeycontribution_t_kernel(tc, k, mq, wq, l, v_bytes, v_scale, wo, out):
    nc = tc.nc
    with ExitStack() as ctx:
        keep = ctx.enter_context(tc.tile_pool(name="keep", bufs=1))
        stream = ctx.enter_context(tc.tile_pool(name="stream", bufs=1))
        psum = ctx.enter_context(tc.psum_pool(name="psum", bufs=1))
        ctx.enter_context(tc.manual_schedule())

        k_rows = [k[h].rearrange("(p i) d -> p i d", p=P) for h in range(H)]
        v_rows = [v_bytes[h].rearrange("(p i) d -> p i d", p=P) for h in range(H)]
        o_rows = [out[h].rearrange("(p i) d -> p i d", p=P) for h in range(H)]

        k_raw = {}
        v_raw = {}

        def load_k(g, parts=1):
            h, i0 = divmod(g * GROUP, TILES)
            t = stream.tile([P, GROUP, K], BF16, tag="k_raw", name="k_raw", bufs=8, align_bytes=64)
            step = GROUP // parts
            for a in range(0, GROUP, step):
                nc.sync.dma_start(out=t[:, a : a + step, :], in_=k_rows[h][:, i0 + a : i0 + a + step, :])
            k_raw[g] = t

        def load_v(g):
            h, i0 = divmod(g * GROUP, TILES)
            t = stream.tile([P, GROUP, K], U8, tag="v_raw", name="v_raw", bufs=8, align_bytes=64)
            nc.sync.dma_start(out=t[:], in_=v_rows[h][:, i0 : i0 + GROUP, :])
            v_raw[g] = t

        def load_w(src, width, name):
            t = keep.tile([P, 4, width], BF16, name=name, align_bytes=64)
            nc.sync.dma_start(out=t[:], in_=src.rearrange("(p j) c -> p j c", j=4))
            return t

        load_k(0, parts=2)
        mq_raw = keep.tile([P, H, 4], BF16, name="mq_raw", align_bytes=64)
        nc.sync.dma_start(out=mq_raw[:], in_=mq.rearrange("h (p t) -> p h t", t=4))
        wq_raw = {0: load_w(wq[0], D, "wq_raw0")}
        l_raw = load_w(l, R, "l_raw")
        load_k(1)
        scale_row = keep.tile([P, 2 * K], F32, name="scale_row", align_bytes=64)
        nc.sync.dma_start(out=scale_row[:, 0:K], in_=v_scale.rearrange("a b c -> (a b c)").partition_broadcast(P))
        load_v(0)
        load_k(2)
        load_k(3)
        load_v(1)
        wo_raw = {0: load_w(wo[0], D, "wo_raw0")}
        wq_raw[1] = load_w(wq[1], D, "wq_raw1")
        wo_raw[1] = load_w(wo[1], D, "wo_raw1")
        for g in range(4, 8):
            load_k(g)
            load_v(g - 2)
        load_v(6)
        load_v(7)

        ident = keep.tile([P, P], F32, name="ident", align_bytes=64)
        make_identity(nc, ident[:])
        ones = keep.tile([P, P], F32, name="ones", align_bytes=64)
        nc.gpsimd.memset(ones[:], 1.0 / S)
        fold = keep.tile([P, 7 * 32], F32, name="fold", align_bytes=64)
        nc.vector.memset(fold[:], 0.0)
        nc.vector.tensor_reduce(out=fold[:, 96:128], in_=ident[:].rearrange("p (n t) -> p n t", t=4), axis=AX.X, op=ALU.add)
        mask = keep.tile([P, 4], F32, name="mask", align_bytes=64)
        nc.vector.tensor_reduce(out=mask[:], in_=ident[:].rearrange("p (n t) -> p t n", t=4), axis=AX.X, op=ALU.add)
        mq_wide = keep.tile([P, H, MEAN_N], BF16, name="mq_wide", align_bytes=64)
        nc.vector.memset(mq_wide[:], 0.0)
        nc.vector.tensor_copy(out=mq_wide[:, :, 0:4], in_=mq_raw[:])
        warm = keep.tile([P, 1], F32, name="warm")
        nc.gpsimd.memset(warm[:], 0.0)
        warm_out = keep.tile([P, 1], F32, name="warm_out")
        nc.scalar.activation(out=warm_out[:], in_=warm[:], func=ACT.Exp)

        w_tiles = {}

        def weight_tiles(name, width):
            w_tiles[name] = (
                stream.tile([P, 4 * width], BF16, tag="w_grouped%d" % width, name="w_grouped", bufs=2 if width == D else 1, align_bytes=64),
                keep.tile([P, width], U32, name=name + "_codes", align_bytes=64),
                keep.tile([P, width], U8, name=name + "_scales", align_bytes=64),
            )
            return w_tiles[name][1:]

        def weight_layout(name, raw, permute, lo, hi, engine):
            grouped = w_tiles[name][0][:, 4 * lo : 4 * hi]
            if permute:
                o = grouped.rearrange("p (t m j) -> p t m j", m=P, j=4)
                src = raw[:].rearrange("p j (m t) -> p t m j", t=4)[:, lo // P : hi // P]
            else:
                o = grouped.rearrange("p (c j) -> p c j", j=4)
                src = raw[:, :, lo:hi].rearrange("p j c -> p c j")
            if engine == "v":
                nc.vector.tensor_copy(out=o, in_=src)
            else:
                nc.scalar.copy(out=o, in_=src)

        def weight_quantize(name, lo, hi):
            grouped, codes, scales = w_tiles[name]
            nc.vector.quantize_mx(out=codes[:, lo:hi].bitcast(FP8X4), scales=scales[:, lo:hi], in_=grouped[:, 4 * lo : 4 * hi])

        wq_q = {}
        wo_q = {}

        kg, kc, ug, uc, ub, zb, xk, xv, vb, vg, vc, yb, ob = ({} for i in range(13))
        ssq = {}
        mean_ps = {}
        a_t = {}

        def transposes(words, tag_store, i, bank):
            x = psum.tile([P, 2, 2, P], F32, tag=bank, name="x", bufs=1)
            for j in range(2):
                for u in range(2):
                    base = 256 * j
                    nc.tensor.transpose(x[:, j, u, :], words[:, base + u : base + 256 : 2], ident[:])
            tag_store[i] = x

        def evacuate_words(x, i, store, tag, engine):
            g = stream.tile([P, 1024], BF16, tag=tag, name=tag, bufs=G_BUFS, align_bytes=64)
            o = g[:].bitcast(F32).rearrange("p (j s u) -> p j s u", j=2, u=2)
            src = x[:].rearrange("p j u s -> p j s u")
            if engine == "v":
                nc.vector.tensor_copy(out=o, in_=src)
            else:
                nc.scalar.copy(out=o, in_=src)
            store[i] = g

        def quantize(src, tag, bufs):
            codes = stream.tile([P, 256], U32, tag=tag + "_c", name=tag + "_c", bufs=bufs, align_bytes=64)
            scales = stream.tile([P, 256], U8, tag=tag + "_s", name=tag + "_s", bufs=bufs, align_bytes=64)
            nc.vector.quantize_mx(out=codes[:].bitcast(FP8X4), scales=scales[:], in_=src[:])
            return codes, scales

        def k_transpose(i, bank):
            g, half = divmod(2 * i, GROUP)
            words = k_raw[g][:, half : half + 2, :].rearrange("p i d -> p (i d)").bitcast(F32)
            transposes(words, xk, i, bank)

        def v_widen(i):
            g, half = divmod(2 * i, GROUP)
            t = stream.tile([P, 1024], BF16, tag="vb", name="vb", bufs=VB_BUFS, align_bytes=64)
            src = v_raw[g][:, half : half + 2, :].rearrange("p i d -> p (i d)").bitcast(FP8)
            nc.vector.tensor_tensor(out=t[:], in0=src, in1=scale_row[:], op=ALU.mult)
            vb[i] = t

        def mean(i, tag):
            h, j0 = divmod(2 * i, TILES)
            if j0 == 0:
                mean_ps[h] = psum.tile([P, TILES, 4, 4], F32, tag=tag, name="mean", bufs=1)
            for j in range(2):
                for c in range(4):
                    col = 512 * j + P * c
                    at = 16 * (j0 + j) + 4 * c
                    n = min(MEAN_N, 512 - at)
                    bank = mean_ps[h][:].rearrange("p i c t -> p (i c t)")
                    nc.tensor.matmul(bank[:, at : at + n], lhsT=kg[i][:, col : col + P], rhs=mq_wide[:, h, 0:n], start=True, stop=True)

        def u_matmul(i, j, tag):
            h = i // HEAD_PAIRS
            codes, scales = wq_q[h]
            kcodes, kscales = kc[i]
            bank = psum.tile([P, 4, P], F32, tag=tag, name="u", bufs=1)
            for t in range(4):
                nc.tensor.matmul_mx(
                    out=bank[:, t, :],
                    lhsT=codes[:, t * P : (t + 1) * P].bitcast(FP8X4),
                    lhsT_scale=scales[:, t * P : (t + 1) * P],
                    rhs=kcodes[:, j * P : (j + 1) * P].bitcast(FP8X4),
                    rhs_scale=kscales[:, j * P : (j + 1) * P],
                    start=True,
                    stop=True,
                )
            ub[2 * i + j] = bank

        def u_evacuate(i, j, engine):
            if i not in ug:
                ug[i] = stream.tile([P, 1024], BF16, tag="ug", name="ug", bufs=UG_BUFS, align_bytes=64)
            o = ug[i][:, 512 * j : 512 * (j + 1)].rearrange("p (s t) -> p s t", t=4)
            src = ub[2 * i + j][:].rearrange("p t s -> p s t")
            if engine == "v":
                nc.vector.tensor_copy(out=o, in_=src)
            else:
                nc.scalar.copy(out=o, in_=src)

        def z_matmul(i, tag):
            codes, scales = uc[i]
            bank = psum.tile([P, 2, R], F32, tag=tag, name="z", bufs=1)
            for j in range(2):
                nc.tensor.matmul_mx(
                    out=bank[:, j, :],
                    lhsT=codes[:, j * P : (j + 1) * P].bitcast(FP8X4),
                    lhsT_scale=scales[:, j * P : (j + 1) * P],
                    rhs=l_codes[:].bitcast(FP8X4),
                    rhs_scale=l_scales[:],
                    start=True,
                    stop=True,
                )
            zb[i] = bank

        def z_square(i):
            h, j0 = divmod(2 * i, TILES)
            if j0 == 0:
                ssq[h] = keep.tile([P, TILES], F32, name="ssq%d" % h, align_bytes=64)
            for j in range(2):
                junk = stream.tile([P, R], F32, tag="junk", name="junk", bufs=2)
                nc.scalar.activation(out=junk[:], in_=zb[i][:, j, :], func=ACT.Square, accum_out=ssq[h][:, j0 + j : j0 + j + 1])

        def y_matmul(i, j, tag):
            h = i // HEAD_PAIRS
            codes, scales = vc[i]
            wcodes, wscales = wo_q[h]
            bank = psum.tile([P, D], F32, tag=tag, name="y_bank", bufs=1)
            nc.tensor.matmul_mx(
                out=bank[:],
                lhsT=codes[:, j * P : (j + 1) * P].bitcast(FP8X4),
                lhsT_scale=scales[:, j * P : (j + 1) * P],
                rhs=wcodes[:].bitcast(FP8X4),
                rhs_scale=wscales[:],
                start=True,
                stop=True,
            )
            yb[2 * i + j] = bank

        def y_evacuate(i, j, engine):
            h, j0 = divmod(2 * i, TILES)
            if i not in ob:
                ob[i] = stream.tile([P, 2, D], F32, tag="o", name="o", bufs=O_BUFS, align_bytes=64)
            o = ob[i]
            col = a_t[h][:, j0 + j : j0 + j + 1]
            if engine == "v":
                nc.vector.tensor_scalar(out=o[:, j, :], in0=yb[2 * i + j][:], scalar1=col, scalar2=None, op0=ALU.mult)
            else:
                nc.scalar.activation(out=o[:, j, :], in_=yb[2 * i + j][:], func=ACT.Copy, scale=col)
            stored.append(i)
            if stored.count(i) == 2:
                nc.sync.dma_start(out=o_rows[h][:, j0 : j0 + 2, :], in_=o[:])

        stored = []

        def softmax_steps(h):
            def small(name, width=1):
                return keep.tile([P, width], F32, name="%s%d" % (name, h), align_bytes=64)

            neg = small("neg", TILES)
            low = small("low")
            lowest = small("lowest")
            prob = small("prob", TILES)
            part = small("part")
            recip = small("recip")
            a_t[h] = small("a", TILES)
            ps = {}

            def s2(tag):
                ps["low"] = psum.tile([P, P], F32, tag=tag, name="ylow", bufs=1)
                nc.tensor.matmul(ps["low"][:], lhsT=low[:].to_broadcast([P, P]), rhs=ident[:], start=True, stop=True)

            def s0():
                nc.vector.scalar_tensor_tensor(
                    out=neg[:], in0=ssq[h][:], scalar=-0.5 / K, in1=mean_sb[h][:], op0=ALU.mult, op1=ALU.subtract
                )

            def s1():
                nc.vector.tensor_reduce(out=low[:], in_=neg[:], axis=AX.X, op=ALU.min)

            def s3():
                nc.vector.tensor_reduce(out=lowest[:], in_=ps["low"][:], axis=AX.X, op=ALU.min)

            def s4():
                nc.scalar.activation(out=prob[:], in_=neg[:], func=ACT.Exp, scale=-1.0, bias=lowest[:], accum_out=part[:])

            def s5(tag):
                ps["sum"] = psum.tile([P, 1], F32, tag=tag, name="ysum", bufs=1)
                nc.tensor.matmul(ps["sum"][:], lhsT=ones[:], rhs=part[:], start=True, stop=True)

            def s6():
                nc.vector.reciprocal(out=recip[:], in_=ps["sum"][:])

            def s7():
                nc.vector.tensor_scalar(out=a_t[h][:], in0=prob[:], scalar1=recip[:], scalar2=None, op0=ALU.mult)

            def v0():
                s0()
                s1()

            def v2():
                s6()
                s7()

            return [v0, s2, s3, s4, s5, v2]

        mean_sb = {}

        def mean_fold(h, tag):
            ps = psum.tile([P, TILES], F32, tag=tag, name="y_mean", bufs=1)
            for c in range(4):
                nc.tensor.matmul(ps[:], lhsT=fold[:, 96 - 32 * c : 224 - 32 * c], rhs=diag[h][:, :, c], start=(c == 0), stop=(c == 3))
            mean_fp[h] = ps

        def mean_scale(h):
            mean_sb[h] = keep.tile([P, TILES], F32, name="mean_sb%d" % h, align_bytes=64)
            nc.vector.tensor_scalar(out=mean_sb[h][:], in0=mean_fp[h][:], scalar1=1.0 / (K**0.5), scalar2=None, op0=ALU.mult)

        mean_fp = {}

        def mean_diagonal(h):
            d = keep.tile([P, TILES, 4], F32, name="diag%d" % h, align_bytes=64)
            nc.vector.tensor_scalar(out=d[:], in0=mean_ps[h][:, :, :, 0], scalar1=mask[:, 0:1], scalar2=None, op0=ALU.mult)
            for t in range(1, 4):
                nc.vector.scalar_tensor_tensor(
                    out=d[:], in0=mean_ps[h][:, :, :, t], scalar=mask[:, t : t + 1], in1=d[:], op0=ALU.mult, op1=ALU.add
                )
            diag[h] = d

        diag = {}

        ops = {}
        banks = {"kg": G_BUFS, "vg": G_BUFS, "ug": UG_BUFS, "kc": 3, "uc": 3, "vb": VB_BUFS, "o": O_BUFS}
        owners = {b: [] for b in banks}

        def op(name, engines, cost, due, deps, emit, takes=(), kind="", ready=0.0, bank=()):
            ops[name] = {"bank": bank, "engines": engines, "cost": cost, "due": due, "deps": deps, "emit": emit, "takes": takes, "kind": kind, "ready": ready}

        wq_q[0] = weight_tiles("wq0", D)
        wo_q[0] = weight_tiles("wo0", D)
        wq_q[1] = weight_tiles("wq1", D)
        l_codes, l_scales = weight_tiles("l", R)
        wo_q[1] = weight_tiles("wo1", D)

        def weight_ops(name, raw, permute, width, due, ready, split):
            step = width // split
            for s in range(split):
                lo, hi = s * step, (s + 1) * step
                op(
                    (name, "lay", s), "vs" if split > 1 else "v", step * 2.4, due, [],
                    lambda e, lo=lo, hi=hi: weight_layout(name, raw, permute, lo, hi, e), ready=ready,
                )
                op((name, "q", s), "v", step * 1.1, due + 300, [(name, "lay", s)], lambda e, lo=lo, hi=hi: weight_quantize(name, lo, hi))
            return [(name, "q", s) for s in range(split)]

        def k_due(i):
            return 3000 + i * K_STEP

        def v_due(i):
            return V0 + (i * V_STEP if i < V_BEND else V_BEND * V_STEP + (i - V_BEND) * V_STEP2)

        def y_due(i):
            return (Y0 + i * Y_STEP) if i < HEAD_PAIRS else Y1 + (i - HEAD_PAIRS) * Y_STEP2

        wq_done = {
            0: weight_ops("wq0", wq_raw[0], True, D, 2500, 4000, 2),
            1: weight_ops("wq1", wq_raw[1], True, D, k_due(11), 9000, 1),
        }
        l_done = weight_ops("l", l_raw, False, R, k_due(1), 4500, 1)
        wo_done = {
            0: weight_ops("wo0", wo_raw[0], False, D, k_due(5), 8500, 1),
            1: weight_ops("wo1", wo_raw[1], False, D, k_due(17), 9500, 1),
        }
        op(
            "scale", "v", 230, v_due(0) - 500, [],
            lambda e: nc.vector.tensor_copy(out=scale_row[:, K : 2 * K], in_=scale_row[:, 0:K]), ready=6500,
        )

        def k_load_ready(i):
            return 3100 if i == 0 else 3400 if i == 1 else 6000 + 500 * (i - 2)

        def start_k(i, bank):
            k_transpose(i, bank)
            if i % 2 and i // 2 + 8 < PAIRS // 2:
                load_k(i // 2 + 8)

        def start_v(i):
            v_widen(i)
            if i % 2 and i // 2 + 8 < PAIRS // 2:
                load_v(i // 2 + 8)

        def set_kc(i):
            kc[i] = quantize(kg[i], "kq", 3)

        def set_uc(i):
            uc[i] = quantize(ug[i], "uq", 3)

        def set_vc(i):
            vc[i] = quantize(vg[i], "vq", PAIRS)

        for i in range(PAIRS):
            h = i // HEAD_PAIRS
            d = k_due(i)
            prev = [("kt", i - 1)] if i else []
            op(("kt", i), "p", 514, d, prev, lambda e, i=i: start_k(i, e), (), "t", k_load_ready(i), [("ke", i)])
            op(("ke", i), "vs", 535, d + 500, [("kt", i)], lambda e, i=i: evacuate_words(xk[i], i, kg, "kg", e), [("kg", [("kq", i), ("mean", i)])])
            op(("kq", i), "v", 285, d + 1000, [("ke", i)], lambda e, i=i: set_kc(i), [("kc", [("u", i, 0), ("u", i, 1)])])
            op(("mean", i), "p", MEAN_W, d + 1200, [("ke", i)] + ([("mean", i - 1)] if i else []), lambda e, i=i: mean(i, e), (), "m", 0.0, [("diag", h)] if i % HEAD_PAIRS == 0 else ())
            for j in range(2):
                op(("u", i, j), "p", 297, d + 1500 + 250 * j, [("kq", i)] + wq_done[h], lambda e, i=i, j=j: u_matmul(i, j, e), (), "m", 0.0, [("ue", i, j)])
                takes = [("ug", [("uq", i)])] if j == 0 else []
                op(("ue", i, j), "vs", 535, d + 2000 + 250 * j, [("u", i, j)] + ([("ue", i, 0)] if j else []), lambda e, i=i, j=j: u_evacuate(i, j, e), takes)
            op(("uq", i), "v", 285, d + 2600, [("ue", i, 0), ("ue", i, 1)], lambda e, i=i: set_uc(i), [("uc", [("z", i)])])
            op(("z", i), "p", 270, d + 3000, [("uq", i)] + l_done, lambda e, i=i: z_matmul(i, e), (), "m", 0.0, [("zs", i)])
            op(("zs", i), "s", 620, d + 3300, [("z", i)], lambda e, i=i: z_square(i))

            d = v_due(i)
            op(("vw", i), "v", 1045, d, ["scale"], lambda e, i=i: start_v(i), [("vb", [("vt", i)])], "", 7000 + 500 * i)
            op(("vt", i), "p", 514, d + 1300, [("vw", i)], lambda e, i=i: transposes(vb[i][:].bitcast(F32), xv, i, e), (), "t", 0.0, [("ve", i)])
            op(("ve", i), "vs", 535, d + 1900, [("vt", i)], lambda e, i=i: evacuate_words(xv[i], i, vg, "vg", e), [("vg", [("vq", i)])])
            op(("vq", i), "v", 285, d + 2500, [("ve", i)], lambda e, i=i: set_vc(i))

            d = y_due(i)
            for j in range(2):
                order = [("y", i, j - 1)] if j else ([("y", i - 1, 1)] if i else [])
                op(("y", i, j), "p", 265, d + 250 * j, [("vq", i), ("a", h)] + order + wo_done[h], lambda e, i=i, j=j: y_matmul(i, j, e), (), "m", 0.0, [("ye", i, j)])
                takes = [("o", [("ye", i, 1)])] if j == 0 else []
                op(("ye", i, j), "vs", 545, d + 300 + 250 * j, [("y", i, j)] + ([("ye", i, 0)] if j else []), lambda e, i=i, j=j: y_evacuate(i, j, e), takes)

        for h in range(H):
            b = HEAD_PAIRS * (h + 1) - 1
            d = k_due(b) + 1700
            s = softmax_steps(h)
            op(("diag", h), "v", 640, d, [("mean", b)], lambda e, h=h: mean_diagonal(h))
            op(("fold", h), "p", 1100, d + 2000, [("diag", h)], lambda e, h=h: mean_fold(h, e), (), "m", 0.0, [("mscale", h)])
            op(("mscale", h), "v", 60, d + 2500, [("fold", h)], lambda e, h=h: mean_scale(h))
            op(("s0", h), "v", 130, d + 3000, [("mscale", h), ("zs", b)], lambda e, s=s: s[0]())
            op(("s2", h), "p", 300, d + 3200, [("s0", h)], lambda e, s=s: s[1](e), (), "m", 0.0, [("s3", h)])
            op(("s3", h), "v", 150, d + 3400, [("s2", h)], lambda e, s=s: s[2]())
            op(("s4", h), "s", 150, d + 3600, [("s3", h)], lambda e, s=s: s[3]())
            op(("s5", h), "p", 300, d + 3800, [("s4", h)], lambda e, s=s: s[4](e), (), "m", 0.0, [("a", h)])
            op(("a", h), "v", 120, d + 4000, [("s5", h)], lambda e, s=s: s[5]())

        free = {"p": 0.0, "v": 0.0, "s": 0.0}
        last = {"p": None, "v": None, "s": None}
        last_kind = ["m"]
        done = {}
        where = {}

        psum_users = [[] for b in range(8)]

        def users_done(users):
            if [u for u in users if u not in done]:
                return None
            return max([done[u] + HOP for u in users], default=0.0)

        def slot_ready(bank):
            own = owners[bank]
            if len(own) < banks[bank]:
                return 0.0
            return users_done(own[len(own) - banks[bank]])

        def start_time(name, e):
            o = ops[name]
            t = max(free[e], o["ready"])
            for dep in o["deps"]:
                if dep not in done:
                    return None, None
                hop = 0.0 if where[dep] == e else (HOP_P if where[dep] == "p" else HOP)
                if dep == last[e] and e in "vs":
                    hop = ADJACENT
                t = max(t, done[dep] + hop)
            for bank, users in o["takes"]:
                r = slot_ready(bank)
                if r is None:
                    return None, None
                t = max(t, r)
            tag = None
            if o["bank"]:
                free_banks = [(r, b) for b, r in enumerate([users_done(u) for u in psum_users]) if r is not None]
                kinds = ["x" if b[0][0] in ("ke", "ve") else b[0][0] for b in psum_users if b and users_done(b) is None]
                kind = "x" if name[0] in ("kt", "vt") else o["bank"][0][0]
                if kinds.count(kind) >= LIMIT.get(kind, 8):
                    return None, None
                if not free_banks:
                    return None, None
                early = [c for c in free_banks if c[0] <= t]
                r, tag = max(early) if early else min(free_banks)
                t = max(t, r)
            return t, tag

        waiting = list(ops)
        while waiting:
            choices = []
            for name in waiting:
                o = ops[name]
                for e in o["engines"]:
                    t, tag = start_time(name, e)
                    if t is not None:
                        due = o["due"]
                        if e == "p" and o["kind"] != last_kind[0]:
                            t += SWITCH
                            due += SWITCH_DUE
                        if e == "v" and o["engines"] == "vs":
                            due += V_BIAS
                        choices.append((t, due, e, name, tag))
            first = min(choices, key=lambda c: c[:2])
            t, due, e, name, tag = min([c for c in choices if c[2] == first[2] and c[0] <= first[0] + SLACK], key=lambda c: (c[1], c[0]))
            o = ops[name]
            for bank, users in o["takes"]:
                owners[bank].append(users)
            if o["bank"]:
                psum_users[tag] = o["bank"]
            if e == "p":
                last_kind[0] = o["kind"]
            o["emit"]("b%d" % tag if o["bank"] else e)
            done[name] = t + o["cost"]
            free[e] = done[name]
            last[e] = name
            where[name] = e
            waiting.remove(name)
